import numpy as np
import ml_dtypes


def mxq(x, axis, fmt="e4m3"):
    dtype, down = {"e4m3": (ml_dtypes.float8_e4m3fn, 7), "e5m2": (ml_dtypes.float8_e5m2, 14)}[fmt]
    v = np.moveaxis(np.asarray(x, np.float32).astype(ml_dtypes.bfloat16).astype(np.float64), axis, -1)
    blocks = v.reshape(v.shape[:-1] + (-1, 32))
    amax = np.abs(blocks).max(-1, keepdims=True)
    byte = np.maximum(np.where(amax > 0, np.frexp(amax)[1] - 1 + 127, 0) - down, 1)
    scale = np.exp2(byte - 127.0)
    codes = (blocks / scale).astype(np.float32).astype(dtype).astype(np.float64)
    return np.moveaxis((codes * scale).reshape(v.shape), -1, axis)


WIDE = False


def mx_kscale(k):
    if not WIDE:
        return np.ones(k)
    levels = np.array([30, -30])
    if k % 512:
        return np.exp2(np.random.permutation(np.resize(levels, k // 32))).repeat(32)
    a = np.empty((k // 512, 16))
    for p in range(k // 512):
        a[p, :8] = np.random.permutation(np.resize(levels, 8))
        for g in range(8):
            far = levels[np.abs(levels - a[p, g]) >= 10]
            a[p, g + 8] = far[np.random.randint(len(far))]
    return np.exp2(a.ravel()).repeat(32)


def f64(x):
    return np.asarray(x).astype(np.float64)


def striped(idx):
    return np.tile(np.asarray(idx).reshape(-1, 16).T, (8, 1)).astype(np.uint16)


def unstriped(offs):
    return offs[:16].T.reshape(-1).astype(np.int64)


E2M1 = np.array([0.0, 0.5, 1.0, 1.5, 2.0, 3.0, 4.0, 6.0, -0.0, -0.5, -1.0, -1.5, -2.0, -3.0, -4.0, -6.0])


def pack_weight(w, fmt):
    k, n = w.shape
    w = f64(np.asarray(w, np.float32).astype(ml_dtypes.bfloat16)).reshape(k // 32, 32, n)
    amax = np.abs(w).max(1)
    if fmt == "e4m3":
        byte = np.frexp(amax)[1] - 1 + 127 - 7
    else:
        mant, ex = np.frexp(amax / 6.0)
        byte = np.where(mant > 0.5, ex, ex - 1) + 127
    byte = np.clip(np.where(amax > 0, byte, 1), 1, 254)
    scaled = (w * np.exp2(127.0 - byte)[:, None, :]).reshape(k, n).astype(np.float32)
    by_word = np.ascontiguousarray(scaled.reshape(k // 512, 128, 4, n).transpose(0, 1, 3, 2))
    if fmt == "e4m3":
        words = by_word.astype(ml_dtypes.float8_e4m3fn).view(np.uint8)
    else:
        c = by_word.astype(ml_dtypes.float4_e2m1fn).view(np.uint8) & 0xF
        words = (c[..., 0::2] | (c[..., 1::2] << 4)).reshape(k // 512, 128, 2 * n)
    return np.ascontiguousarray(words), np.ascontiguousarray(byte.astype(np.uint8).reshape(k // 512, 16, n))


def unpack_weight(words, scales, fmt):
    g, _, n = scales.shape
    words = np.ascontiguousarray(words).reshape(g, 128, n, -1)
    if fmt == "e4m3":
        vals = words.view(ml_dtypes.float8_e4m3fn).astype(np.float64)
    else:
        nib = np.empty((g, 128, n, 4), np.uint8)
        nib[..., 0::2] = words & 0xF
        nib[..., 1::2] = words >> 4
        vals = E2M1[nib]
    vals = vals * np.repeat(np.exp2(scales.astype(np.float64) - 127.0), 8, axis=1)[..., None]
    return vals.transpose(0, 1, 3, 2).reshape(g * 512, n)


def bf(x):
    return np.asarray(x, np.float32).astype(ml_dtypes.bfloat16)


def planes(Y):
    r, m = Y.shape
    b = f64(bf(Y)).reshape(r // 32, 32, m)
    amax = np.abs(b).max(1)
    byte = np.clip(np.where(amax > 0, np.frexp(amax)[1] - 1 + 127 - 7, 1), 1, 254)
    codes = (b * np.exp2(127.0 - byte)[:, None, :]).reshape(r, m).astype(np.float32).astype(ml_dtypes.float8_e4m3fn).view(np.uint8)
    words = codes.reshape(r // 512, 128, 4, m).transpose(0, 1, 3, 2)
    return np.ascontiguousarray(words), np.ascontiguousarray(byte.astype(np.uint8).reshape(r // 512, 16, m))


K, T, C, J, N = 512, 512, 2048, 512, 512


def setup_inputs():
    n = np.random.standard_normal
    idx = np.random.permutation(C)[:J]
    fk = mx_kscale(K)
    fj = mx_kscale(J)
    tq = np.exp(2 * n((T, J)))
    xtp = pack_weight(n((K, T)) * 0.3 / fk[:, None], "e2m1")
    wcp = pack_weight(n((K, C)) * 1 / np.sqrt(K) * fk[:, None], "e4m3")
    wop = pack_weight(n((J, N)) * 1 / np.sqrt(J) / fj[:, None], "e2m1")
    return {
        "xt_words": xtp[0],
        "xt_scales": xtp[1],
        "wc_words": wcp[0],
        "wc_scales": wcp[1],
        "tg": (tq / tq.sum(axis=1, keepdims=True)).astype(np.float32),
        "fj": (np.random.uniform(16.0, 32.0, (J, 1)) * fj[:, None]).astype(np.float32),
        "wo_words": wop[0],
        "wo_scales": wop[1],
        "offs": striped(idx),
    }


def reference(xt_words, xt_scales, wc_words, wc_scales, tg, fj, wo_words, wo_scales, offs):
    idx = unstriped(offs)
    xtu = unpack_weight(xt_words, xt_scales, "e2m1")
    wcu = unpack_weight(wc_words, wc_scales, "e4m3")
    wou = unpack_weight(wo_words, wo_scales, "e2m1")
    wcidxg = wcu[:, idx]
    z = xtu.T @ wcidxg
    p = np.exp(z)
    d = p / np.sum(p, axis=1, keepdims=True) - f64(tg)
    dt = d.T
    dw = dt * f64(fj)
    dwq = mxq(dw, 0, "e5m2")
    y = wou.T @ dwq
    words, scales = planes(y)
    return y, words, scales

@@ -1,0 +1,179 @@
+from contextlib import ExitStack
+
+import concourse.mybir as mybir
+from concourse.masks import make_identity
+
+K, T, C, J, N = 512, 512, 2048, 512, 512
+FLOPS = 2 * K * T * J + 2 * J * N * T
+
+F32 = mybir.dt.float32
+BF16 = mybir.dt.bfloat16
+I32 = mybir.dt.int32
+U32 = mybir.dt.uint32
+U16 = mybir.dt.uint16
+U8 = mybir.dt.uint8
+E4M3 = mybir.dt.float8_e4m3fn_x4
+E5M2 = mybir.dt.float8_e5m2_x4
+E2M1 = mybir.dt.float4_e2m1fn_x4
+ALU = mybir.AluOpType
+ACT = mybir.ActivationFunctionType
+AX = mybir.AxisListType
+
+P = 128
+PACK = 4
+TILES = T // P
+
+
+def load_scale_rows(queue, plane, rows):
+    for q in range(4):
+        queue.dma_start(out=plane[32 * q : 32 * q + 4, :].bitcast(I32), in_=rows[0, 4 * q : 4 * q + 4, :].bitcast(I32))
+
+
+def tile_list_class_error_back_pl_kernel(
+    tc, xt_words, xt_scales, wc_words, wc_scales, tg, fj, wo_words, wo_scales, offs, out_0, out_1, out_2
+):
+    nc = tc.nc
+    with ExitStack() as ctx:
+        keep = ctx.enter_context(tc.tile_pool(name="keep", bufs=1))
+        work = ctx.enter_context(tc.tile_pool(name="work", bufs=TILES))
+        z_banks = ctx.enter_context(tc.psum_pool(name="z_banks", bufs=TILES))
+        turn_banks = ctx.enter_context(tc.psum_pool(name="turn_banks", bufs=2))
+        y_banks = ctx.enter_context(tc.psum_pool(name="y_banks", bufs=2))
+
+        offsets = keep.tile([P, J // 16], U16, name="offsets")
+        nc.sync.dma_start(offsets[:], offs)
+        wc_codes = keep.tile([P, C], I32, name="wc_codes", align_bytes=64)
+        nc.sync.dma_start(out=wc_codes[:], in_=wc_words[0].rearrange("p c r -> p (c r)").bitcast(I32))
+        wc_plane = keep.tile([P, C], U8, name="wc_plane", align_bytes=64)
+        nc.vector.memset(wc_plane[:].bitcast(I32), 0)
+        load_scale_rows(nc.scalar, wc_plane, wc_scales)
+        xt_codes = keep.tile([P, 2 * T], U8, name="xt_codes", align_bytes=64)
+        nc.sync.dma_start(out=xt_codes[:].bitcast(I32), in_=xt_words[0].bitcast(I32))
+        targets = keep.tile([P, TILES, J], F32, name="targets")
+        nc.sync.dma_start(out=targets[:], in_=tg.rearrange("(k p) j -> p k j", p=P))
+
+        ident = keep.tile([P, P], F32, name="ident")
+        make_identity(nc, ident[:])
+        wo_plane = keep.tile([P, N], U8, name="wo_plane", align_bytes=64)
+        nc.gpsimd.memset(wo_plane[:].bitcast(I32), 0)
+        load_scale_rows(nc.sync, wo_plane, wo_scales)
+        fj_rows = keep.tile([P, PACK], F32, name="fj_rows")
+        nc.gpsimd.dma_start(out=fj_rows[:], in_=fj.rearrange("(p i) o -> p (i o)", i=PACK))
+        xt_plane = keep.tile([P, T], U8, name="xt_plane", align_bytes=64)
+        nc.gpsimd.memset(xt_plane[:].bitcast(I32), 0)
+        load_scale_rows(nc.scalar, xt_plane, xt_scales)
+        wo_codes = keep.tile([P, 2 * N], U8, name="wo_codes", align_bytes=64)
+        nc.gpsimd.dma_start(out=wo_codes[:].bitcast(I32), in_=wo_words[0].bitcast(I32))
+
+        picked_plane = keep.tile([P, J], U8, name="picked_plane", align_bytes=64)
+        nc.vector.tensor_copy(picked_plane[:], wc_plane[:].indirect(offsets[:]))
+        picked_codes = keep.tile([P, J], U32, name="picked_codes", align_bytes=64)
+        nc.vector.tensor_copy(picked_codes[:], wc_codes[:].bitcast(U32).indirect(offsets[:]))
+
+        fj_bank = turn_banks.tile([P, PACK, P], F32, name="turned", tag="turned")
+        for i in range(PACK):
+            nc.tensor.transpose(fj_bank[:, i, :], fj_rows[:, i : i + 1].to_broadcast([P, P]), ident[:])
+        minus_fj = keep.tile([P, P, PACK], F32, name="minus_fj")
+        nc.scalar.activation(out=minus_fj[:], in_=fj_bank[:].rearrange("p i q -> p q i"), func=ACT.Copy, scale=-1.0)
+
+        wo_dealt_codes = keep.tile([P, 2 * N], U8, name="wo_dealt_codes", align_bytes=64)
+        nc.vector.tensor_copy(
+            out=wo_dealt_codes[:].bitcast(U16).rearrange("p (i q) -> p i q", i=PACK),
+            in_=wo_codes[:].bitcast(U16).rearrange("p (q i) -> p i q", i=PACK),
+        )
+        wo_dealt_plane = keep.tile([P, N], U8, name="wo_dealt_plane", align_bytes=64)
+        nc.vector.tensor_copy(
+            out=wo_dealt_plane[:].rearrange("p (i q) -> p i q", i=PACK),
+            in_=wo_plane[:].rearrange("p (q i) -> p i q", i=PACK),
+        )
+
+        y_codes = keep.tile([P, T], U32, name="y_codes", align_bytes=64)
+        y_plane = keep.tile([P, T], U8, name="y_plane", align_bytes=64)
+        out_rows = out_0.rearrange("(p i) t -> p i t", i=PACK)
+        out_codes = out_1[0].rearrange("p t r -> p (t r)").bitcast(I32)
+        exps, sums, grouped, rounded = {}, {}, {}, {}
+
+        def shares(k):
+            z = z_banks.tile([P, J], F32, name="z")
+            nc.tensor.matmul_mx(
+                out=z[:],
+                lhsT=xt_codes[:, 2 * P * k : 2 * P * (k + 1)].bitcast(E2M1),
+                lhsT_scale=xt_plane[:, P * k : P * (k + 1)],
+                rhs=picked_codes[:].bitcast(E4M3),
+                rhs_scale=picked_plane[:],
+                start=True,
+                stop=True,
+            )
+            minus_top = work.tile([P, 1], F32, name="minus_top")
+            nc.vector.tensor_reduce(out=minus_top[:], in_=z[:], axis=AX.X, op=ALU.max, negate=True)
+            exps[k] = work.tile([P, J], F32, name="exps")
+            sums[k] = work.tile([P, 1], F32, name="sums")
+            nc.scalar.activation(out=exps[k][:], in_=z[:], func=ACT.Exp, bias=minus_top[:], accum_out=sums[k][:])
+
+        def errors(k):
+            gap = work.tile([P, J], F32, name="gap")
+            nc.vector.scalar_tensor_tensor(
+                out=gap[:], in0=targets[:, k, :], scalar=sums[k][:], in1=exps[k][:], op0=ALU.mult, op1=ALU.subtract
+            )
+            inverse = work.tile([P, 1], F32, name="inverse")
+            nc.vector.reciprocal(out=inverse[:], in_=sums[k][:])
+            dw = work.tile([P, J], BF16, name="dw")
+            nc.vector.scalar_tensor_tensor(
+                out=dw[:],
+                in0=gap[:],
+                scalar=inverse[:],
+                in1=minus_fj[:].rearrange("p q i -> p (q i)"),
+                op0=ALU.mult,
+                op1=ALU.mult,
+            )
+            pairs = dw[:].bitcast(F32)
+            turned = turn_banks.tile([P, PACK, P], F32, name="turned", tag="turned")
+            for u in range(2):
+                nc.tensor.transpose(turned[:, u, :], pairs[:, u : J // 2 : 2], ident[:])
+            grouped[k] = work.tile([P, P * PACK], BF16, name="grouped", align_bytes=64)
+            nc.scalar.copy(
+                out=grouped[k][:].bitcast(F32).rearrange("p (t u) -> p t u", u=2),
+                in_=turned[:, 0:2, :].rearrange("p u t -> p t u"),
+            )
+
+        def back(k):
+            dw_codes = work.tile([P, P], U32, name="dw_codes", align_bytes=64)
+            dw_plane = work.tile([P, P], U8, name="dw_plane", align_bytes=64)
+            nc.vector.quantize_mx(out=dw_codes[:].bitcast(E5M2), scales=dw_plane[:], in_=grouped[k][:])
+            y = y_banks.tile([P, PACK, P], F32, name="y")
+            for i in range(PACK):
+                nc.tensor.matmul_mx(
+                    out=y[:, i, :],
+                    lhsT=wo_dealt_codes[:, 2 * P * i : 2 * P * (i + 1)].bitcast(E2M1),
+                    lhsT_scale=wo_dealt_plane[:, P * i : P * (i + 1)],
+                    rhs=dw_codes[:].bitcast(E5M2),
+                    rhs_scale=dw_plane[:],
+                    start=True,
+                    stop=True,
+                )
+            result = work.tile([P, PACK, P], F32, name="result")
+            nc.scalar.copy(out=result[:], in_=y[:])
+            nc.sync.dma_start(out=out_rows[:, :, P * k : P * (k + 1)], in_=result[:])
+            rounded[k] = work.tile([P, P, PACK], BF16, name="rounded", align_bytes=64)
+            nc.scalar.copy(out=rounded[k][:], in_=y[:].rearrange("p i t -> p t i"))
+
+        def planes(k):
+            cols = slice(P * k, P * (k + 1))
+            nc.vector.quantize_mx(
+                out=y_codes[:, cols].bitcast(E4M3),
+                scales=y_plane[:, cols],
+                in_=rounded[k][:].rearrange("p t i -> p (t i)"),
+            )
+            nc.sync.dma_start(out=out_codes[:, cols], in_=y_codes[:, cols].bitcast(I32))
+
+        stages = (shares, errors, back, planes)
+        for step in range(TILES + len(stages) - 1):
+            for depth, stage in enumerate(stages):
+                if 0 <= step - depth < TILES:
+                    stage(step - depth)
+
+        for q in range(4):
+            queue = nc.sync if q % 2 == 0 else nc.scalar
+            queue.dma_start(
+                out=out_2[0, 4 * q : 4 * q + 4, :].bitcast(I32), in_=y_plane[32 * q : 32 * q + 4, :].bitcast(I32)
+            )

@@ -22,10 +22,12 @@ AX = mybir.AxisListType
 P = 128
 PACK = 4
 TILES = T // P
+LEAD = C // 2
+EARLY = 2
 
 
-def load_scale_rows(queue, plane, rows):
-    for q in range(4):
+def load_scale_rows(queues, plane, rows):
+    for q, queue in enumerate(queues):
         queue.dma_start(out=plane[32 * q : 32 * q + 4, :].bitcast(I32), in_=rows[0, 4 * q : 4 * q + 4, :].bitcast(I32))
 
 
@@ -36,45 +38,46 @@ def tile_list_class_error_back_pl_kernel(
     with ExitStack() as ctx:
         keep = ctx.enter_context(tc.tile_pool(name="keep", bufs=1))
         work = ctx.enter_context(tc.tile_pool(name="work", bufs=TILES))
-        z_banks = ctx.enter_context(tc.psum_pool(name="z_banks", bufs=TILES))
-        turn_banks = ctx.enter_context(tc.psum_pool(name="turn_banks", bufs=2))
-        y_banks = ctx.enter_context(tc.psum_pool(name="y_banks", bufs=2))
+        banks = ctx.enter_context(tc.psum_pool(name="banks", bufs=1))
+
+        def bank(number, shape):
+            return banks.tile(shape, F32, name="bank%d" % number, tag="bank%d" % number)
 
         offsets = keep.tile([P, J // 16], U16, name="offsets")
         nc.sync.dma_start(offsets[:], offs)
+        wc_rows = wc_words[0].rearrange("p c r -> p (c r)").bitcast(I32)
         wc_codes = keep.tile([P, C], I32, name="wc_codes", align_bytes=64)
-        nc.sync.dma_start(out=wc_codes[:], in_=wc_words[0].rearrange("p c r -> p (c r)").bitcast(I32))
+        nc.sync.dma_start(out=wc_codes[:, 0:LEAD], in_=wc_rows[:, 0:LEAD])
         wc_plane = keep.tile([P, C], U8, name="wc_plane", align_bytes=64)
         nc.vector.memset(wc_plane[:].bitcast(I32), 0)
-        load_scale_rows(nc.scalar, wc_plane, wc_scales)
+        load_scale_rows([nc.sync, nc.sync, nc.scalar, nc.scalar], wc_plane, wc_scales)
+        nc.sync.dma_start(out=wc_codes[:, LEAD:C], in_=wc_rows[:, LEAD:C])
         xt_codes = keep.tile([P, 2 * T], U8, name="xt_codes", align_bytes=64)
         nc.sync.dma_start(out=xt_codes[:].bitcast(I32), in_=xt_words[0].bitcast(I32))
-        targets = keep.tile([P, TILES, J], F32, name="targets")
-        nc.sync.dma_start(out=targets[:], in_=tg.rearrange("(k p) j -> p k j", p=P))
-
+        wo_codes = keep.tile([P, 2 * N], U8, name="wo_codes", align_bytes=64)
+        nc.sync.dma_start(out=wo_codes[:].bitcast(I32), in_=wo_words[0].bitcast(I32))
+        xt_plane = keep.tile([P, T], U8, name="xt_plane", align_bytes=64)
+        nc.vector.memset(xt_plane[:].bitcast(I32), 0)
+        load_scale_rows([nc.sync] * 4, xt_plane, xt_scales)
+        targets = [work.tile([P, J], F32, name="targets") for k in range(TILES)]
+        for k in range(TILES - 1):
+            nc.sync.dma_start(out=targets[k][:], in_=tg[P * k : P * (k + 1), :])
+        fj_rows = keep.tile([P, PACK], F32, name="fj_rows")
+        nc.sync.dma_start(out=fj_rows[:], in_=fj.rearrange("(p i) o -> p (i o)", i=PACK))
+        wo_plane = keep.tile([P, N], U8, name="wo_plane", align_bytes=64)
+        nc.vector.memset(wo_plane[:].bitcast(I32), 0)
+        load_scale_rows([nc.sync] * 4, wo_plane, wo_scales)
+        nc.sync.dma_start(out=targets[TILES - 1][:], in_=tg[P * (TILES - 1) : T, :])
         ident = keep.tile([P, P], F32, name="ident")
         make_identity(nc, ident[:])
-        wo_plane = keep.tile([P, N], U8, name="wo_plane", align_bytes=64)
-        nc.gpsimd.memset(wo_plane[:].bitcast(I32), 0)
-        load_scale_rows(nc.sync, wo_plane, wo_scales)
-        fj_rows = keep.tile([P, PACK], F32, name="fj_rows")
-        nc.gpsimd.dma_start(out=fj_rows[:], in_=fj.rearrange("(p i) o -> p (i o)", i=PACK))
-        xt_plane = keep.tile([P, T], U8, name="xt_plane", align_bytes=64)
-        nc.gpsimd.memset(xt_plane[:].bitcast(I32), 0)
-        load_scale_rows(nc.scalar, xt_plane, xt_scales)
-        wo_codes = keep.tile([P, 2 * N], U8, name="wo_codes", align_bytes=64)
-        nc.gpsimd.dma_start(out=wo_codes[:].bitcast(I32), in_=wo_words[0].bitcast(I32))
 
         picked_plane = keep.tile([P, J], U8, name="picked_plane", align_bytes=64)
         nc.vector.tensor_copy(picked_plane[:], wc_plane[:].indirect(offsets[:]))
+        halves = [slice(0, J // 2), slice(J // 2, J)]
         picked_codes = keep.tile([P, J], U32, name="picked_codes", align_bytes=64)
-        nc.vector.tensor_copy(picked_codes[:], wc_codes[:].bitcast(U32).indirect(offsets[:]))
-
-        fj_bank = turn_banks.tile([P, PACK, P], F32, name="turned", tag="turned")
-        for i in range(PACK):
-            nc.tensor.transpose(fj_bank[:, i, :], fj_rows[:, i : i + 1].to_broadcast([P, P]), ident[:])
-        minus_fj = keep.tile([P, P, PACK], F32, name="minus_fj")
-        nc.scalar.activation(out=minus_fj[:], in_=fj_bank[:].rearrange("p i q -> p q i"), func=ACT.Copy, scale=-1.0)
+        for cols in halves:
+            entries = offsets[:, cols.start // 16 : cols.stop // 16]
+            nc.vector.tensor_copy(picked_codes[:, cols], wc_codes[:].bitcast(U32).indirect(entries))
 
         wo_dealt_codes = keep.tile([P, 2 * N], U8, name="wo_dealt_codes", align_bytes=64)
         nc.vector.tensor_copy(
@@ -91,59 +94,72 @@ def tile_list_class_error_back_pl_kernel(
         y_plane = keep.tile([P, T], U8, name="y_plane", align_bytes=64)
         out_rows = out_0.rearrange("(p i) t -> p i t", i=PACK)
         out_codes = out_1[0].rearrange("p t r -> p (t r)").bitcast(I32)
-        exps, sums, grouped, rounded = {}, {}, {}, {}
+        z, exps, sums, dealt, turned, grouped, y, result, rounded = {}, {}, {}, {}, {}, {}, {}, {}, {}
 
-        def shares(k):
-            z = z_banks.tile([P, J], F32, name="z")
-            nc.tensor.matmul_mx(
-                out=z[:],
-                lhsT=xt_codes[:, 2 * P * k : 2 * P * (k + 1)].bitcast(E2M1),
-                lhsT_scale=xt_plane[:, P * k : P * (k + 1)],
-                rhs=picked_codes[:].bitcast(E4M3),
-                rhs_scale=picked_plane[:],
-                start=True,
-                stop=True,
-            )
+        def exponentials(k):
+            z[k] = bank(k, [P, J])
+            for cols in halves if k == 0 else [slice(0, J)]:
+                nc.tensor.matmul_mx(
+                    out=z[k][:, cols],
+                    lhsT=xt_codes[:, 2 * P * k : 2 * P * (k + 1)].bitcast(E2M1),
+                    lhsT_scale=xt_plane[:, P * k : P * (k + 1)],
+                    rhs=picked_codes[:, cols].bitcast(E4M3),
+                    rhs_scale=picked_plane[:, cols],
+                    start=True,
+                    stop=True,
+                )
             minus_top = work.tile([P, 1], F32, name="minus_top")
-            nc.vector.tensor_reduce(out=minus_top[:], in_=z[:], axis=AX.X, op=ALU.max, negate=True)
-            exps[k] = work.tile([P, J], F32, name="exps")
+            nc.vector.tensor_reduce(out=minus_top[:], in_=z[k][:], axis=AX.X, op=ALU.max, negate=True)
+            exps[k] = work.tile([P, PACK, P], F32, name="exps")
             sums[k] = work.tile([P, 1], F32, name="sums")
-            nc.scalar.activation(out=exps[k][:], in_=z[:], func=ACT.Exp, bias=minus_top[:], accum_out=sums[k][:])
-
-        def errors(k):
-            gap = work.tile([P, J], F32, name="gap")
-            nc.vector.scalar_tensor_tensor(
-                out=gap[:], in0=targets[:, k, :], scalar=sums[k][:], in1=exps[k][:], op0=ALU.mult, op1=ALU.subtract
+            nc.scalar.activation(
+                out=exps[k][:],
+                in_=z[k][:].rearrange("p (q i) -> p i q", i=PACK),
+                func=ACT.Exp,
+                bias=minus_top[:],
+                accum_out=sums[k][:],
             )
+
+        def deal_targets(k):
+            dealt[k] = work.tile([P, PACK, P], F32, name="dealt")
+            nc.scalar.copy(
+                out=dealt[k][:].rearrange("p i q -> p q i"), in_=targets[k][:].rearrange("p (q i) -> p q i", i=PACK)
+            )
+
+        def gaps(k):
             inverse = work.tile([P, 1], F32, name="inverse")
             nc.vector.reciprocal(out=inverse[:], in_=sums[k][:])
-            dw = work.tile([P, J], BF16, name="dw")
+            gap = work.tile([P, PACK, P], F32, name="gap")
             nc.vector.scalar_tensor_tensor(
-                out=dw[:],
-                in0=gap[:],
-                scalar=inverse[:],
-                in1=minus_fj[:].rearrange("p q i -> p (q i)"),
-                op0=ALU.mult,
-                op1=ALU.mult,
+                out=gap[:], in0=exps[k][:], scalar=inverse[:], in1=dealt[k][:], op0=ALU.mult, op1=ALU.subtract
             )
-            pairs = dw[:].bitcast(F32)
-            turned = turn_banks.tile([P, PACK, P], F32, name="turned", tag="turned")
-            for u in range(2):
-                nc.tensor.transpose(turned[:, u, :], pairs[:, u : J // 2 : 2], ident[:])
-            grouped[k] = work.tile([P, P * PACK], BF16, name="grouped", align_bytes=64)
-            nc.scalar.copy(
-                out=grouped[k][:].bitcast(F32).rearrange("p (t u) -> p t u", u=2),
-                in_=turned[:, 0:2, :].rearrange("p u t -> p t u"),
+            turned[k] = bank(TILES + k, [P, PACK, P])
+            for i in range(PACK):
+                nc.tensor.transpose(turned[k][:, i, :], gap[:, i, :], ident[:])
+
+        def errors(k):
+            grouped[k] = work.tile([P, P, PACK], BF16, name="grouped", align_bytes=64)
+            nc.vector.tensor_tensor(
+                out=grouped[k][:],
+                in0=turned[k][:].rearrange("p i t -> p t i"),
+                in1=fj_rows[:].unsqueeze(1).to_broadcast([P, P, PACK]),
+                op=ALU.mult,
             )
 
         def back(k):
             dw_codes = work.tile([P, P], U32, name="dw_codes", align_bytes=64)
             dw_plane = work.tile([P, P], U8, name="dw_plane", align_bytes=64)
-            nc.vector.quantize_mx(out=dw_codes[:].bitcast(E5M2), scales=dw_plane[:], in_=grouped[k][:])
-            y = y_banks.tile([P, PACK, P], F32, name="y")
+            nc.vector.quantize_mx(out=dw_codes[:].bitcast(E5M2), scales=dw_plane[:], in_=grouped[k][:].rearrange("p t i -> p (t i)"))
+            if k < TILES - 1:
+                whole = bank(k, [P, PACK, P])
+                y[k] = [whole]
+                slots = [whole[:, i, :] for i in range(PACK)]
+            else:
+                y[k] = [bank(k, [P, 2, P]), bank(k + 1, [P, 2, P])]
+                slots = [y[k][i // 2][:, i % 2, :] for i in range(PACK)]
             for i in range(PACK):
                 nc.tensor.matmul_mx(
-                    out=y[:, i, :],
+                    out=slots[i],
                     lhsT=wo_dealt_codes[:, 2 * P * i : 2 * P * (i + 1)].bitcast(E2M1),
                     lhsT_scale=wo_dealt_plane[:, P * i : P * (i + 1)],
                     rhs=dw_codes[:].bitcast(E5M2),
@@ -151,11 +167,19 @@ def tile_list_class_error_back_pl_kernel(
                     start=True,
                     stop=True,
                 )
-            result = work.tile([P, PACK, P], F32, name="result")
-            nc.scalar.copy(out=result[:], in_=y[:])
-            nc.sync.dma_start(out=out_rows[:, :, P * k : P * (k + 1)], in_=result[:])
+
+        def store(k):
+            result[k] = work.tile([P, PACK, P], F32, name="result")
+            if k < TILES - 1:
+                nc.scalar.copy(out=result[k][:], in_=y[k][0][:])
+            else:
+                nc.scalar.copy(out=result[k][:, 0:2, :], in_=y[k][0][:])
+                nc.vector.tensor_copy(out=result[k][:, 2:4, :], in_=y[k][1][:])
+            nc.sync.dma_start(out=out_rows[:, :, P * k : P * (k + 1)], in_=result[k][:])
+
+        def rounding(k):
             rounded[k] = work.tile([P, P, PACK], BF16, name="rounded", align_bytes=64)
-            nc.scalar.copy(out=rounded[k][:], in_=y[:].rearrange("p i t -> p t i"))
+            nc.vector.tensor_copy(out=rounded[k][:], in_=result[k][:].rearrange("p i t -> p t i"))
 
         def planes(k):
             cols = slice(P * k, P * (k + 1))
@@ -164,13 +188,28 @@ def tile_list_class_error_back_pl_kernel(
                 scales=y_plane[:, cols],
                 in_=rounded[k][:].rearrange("p t i -> p (t i)"),
             )
-            nc.sync.dma_start(out=out_codes[:, cols], in_=y_codes[:, cols].bitcast(I32))
+            if k % 2 == 1:
+                pair = slice(P * (k - 1), P * (k + 1))
+                nc.sync.dma_start(out=out_codes[:, pair], in_=y_codes[:, pair].bitcast(I32))
 
-        stages = (shares, errors, back, planes)
-        for step in range(TILES + len(stages) - 1):
-            for depth, stage in enumerate(stages):
-                if 0 <= step - depth < TILES:
-                    stage(step - depth)
+        for k in range(EARLY):
+            deal_targets(k)
+        for k in range(TILES):
+            exponentials(k)
+        for k in range(TILES):
+            if k >= EARLY:
+                deal_targets(k)
+            gaps(k)
+        for step in range(TILES + 1):
+            if step < TILES:
+                errors(step)
+            if step >= 1:
+                back(step - 1)
+        for k in range(TILES):
+            store(k)
+            rounding(k)
+        for k in range(TILES):
+            planes(k)
 
         for q in range(4):
             queue = nc.sync if q % 2 == 0 else nc.scalar

from contextlib import ExitStack

import concourse.mybir as mybir
from concourse.masks import make_identity

K, T, C, J, N = 512, 512, 2048, 512, 512
FLOPS = 2 * K * T * J + 2 * J * N * T

F32 = mybir.dt.float32
BF16 = mybir.dt.bfloat16
I32 = mybir.dt.int32
U32 = mybir.dt.uint32
U16 = mybir.dt.uint16
U8 = mybir.dt.uint8
E4M3 = mybir.dt.float8_e4m3fn_x4
E5M2 = mybir.dt.float8_e5m2_x4
E2M1 = mybir.dt.float4_e2m1fn_x4
ALU = mybir.AluOpType
ACT = mybir.ActivationFunctionType
AX = mybir.AxisListType

P = 128
PACK = 4
TILES = T // P
LEAD = C // 2
EARLY = 2


def load_scale_rows(queues, plane, rows):
    for q, queue in enumerate(queues):
        queue.dma_start(out=plane[32 * q : 32 * q + 4, :].bitcast(I32), in_=rows[0, 4 * q : 4 * q + 4, :].bitcast(I32))


def tile_list_class_error_back_pl_kernel(
    tc, xt_words, xt_scales, wc_words, wc_scales, tg, fj, wo_words, wo_scales, offs, out_0, out_1, out_2
):
    nc = tc.nc
    with ExitStack() as ctx:
        keep = ctx.enter_context(tc.tile_pool(name="keep", bufs=1))
        work = ctx.enter_context(tc.tile_pool(name="work", bufs=TILES))
        banks = ctx.enter_context(tc.psum_pool(name="banks", bufs=1))

        def bank(number, shape):
            return banks.tile(shape, F32, name="bank%d" % number, tag="bank%d" % number)

        offsets = keep.tile([P, J // 16], U16, name="offsets")
        nc.sync.dma_start(offsets[:], offs)
        wc_rows = wc_words[0].rearrange("p c r -> p (c r)").bitcast(I32)
        wc_codes = keep.tile([P, C], I32, name="wc_codes", align_bytes=64)
        nc.sync.dma_start(out=wc_codes[:, 0:LEAD], in_=wc_rows[:, 0:LEAD])
        wc_plane = keep.tile([P, C], U8, name="wc_plane", align_bytes=64)
        nc.vector.memset(wc_plane[:].bitcast(I32), 0)
        load_scale_rows([nc.sync, nc.sync, nc.scalar, nc.scalar], wc_plane, wc_scales)
        nc.sync.dma_start(out=wc_codes[:, LEAD:C], in_=wc_rows[:, LEAD:C])
        xt_codes = keep.tile([P, 2 * T], U8, name="xt_codes", align_bytes=64)
        nc.sync.dma_start(out=xt_codes[:].bitcast(I32), in_=xt_words[0].bitcast(I32))
        wo_codes = keep.tile([P, 2 * N], U8, name="wo_codes", align_bytes=64)
        nc.sync.dma_start(out=wo_codes[:].bitcast(I32), in_=wo_words[0].bitcast(I32))
        xt_plane = keep.tile([P, T], U8, name="xt_plane", align_bytes=64)
        nc.vector.memset(xt_plane[:].bitcast(I32), 0)
        load_scale_rows([nc.sync] * 4, xt_plane, xt_scales)
        targets = [work.tile([P, J], F32, name="targets") for k in range(TILES)]
        for k in range(TILES - 1):
            nc.sync.dma_start(out=targets[k][:], in_=tg[P * k : P * (k + 1), :])
        fj_rows = keep.tile([P, PACK], F32, name="fj_rows")
        nc.sync.dma_start(out=fj_rows[:], in_=fj.rearrange("(p i) o -> p (i o)", i=PACK))
        wo_plane = keep.tile([P, N], U8, name="wo_plane", align_bytes=64)
        nc.vector.memset(wo_plane[:].bitcast(I32), 0)
        load_scale_rows([nc.sync] * 4, wo_plane, wo_scales)
        nc.sync.dma_start(out=targets[TILES - 1][:], in_=tg[P * (TILES - 1) : T, :])
        ident = keep.tile([P, P], F32, name="ident")
        make_identity(nc, ident[:])

        picked_plane = keep.tile([P, J], U8, name="picked_plane", align_bytes=64)
        nc.vector.tensor_copy(picked_plane[:], wc_plane[:].indirect(offsets[:]))
        halves = [slice(0, J // 2), slice(J // 2, J)]
        picked_codes = keep.tile([P, J], U32, name="picked_codes", align_bytes=64)
        for cols in halves:
            entries = offsets[:, cols.start // 16 : cols.stop // 16]
            nc.vector.tensor_copy(picked_codes[:, cols], wc_codes[:].bitcast(U32).indirect(entries))

        wo_dealt_codes = keep.tile([P, 2 * N], U8, name="wo_dealt_codes", align_bytes=64)
        nc.vector.tensor_copy(
            out=wo_dealt_codes[:].bitcast(U16).rearrange("p (i q) -> p i q", i=PACK),
            in_=wo_codes[:].bitcast(U16).rearrange("p (q i) -> p i q", i=PACK),
        )
        wo_dealt_plane = keep.tile([P, N], U8, name="wo_dealt_plane", align_bytes=64)
        nc.vector.tensor_copy(
            out=wo_dealt_plane[:].rearrange("p (i q) -> p i q", i=PACK),
            in_=wo_plane[:].rearrange("p (q i) -> p i q", i=PACK),
        )

        y_codes = keep.tile([P, T], U32, name="y_codes", align_bytes=64)
        y_plane = keep.tile([P, T], U8, name="y_plane", align_bytes=64)
        out_rows = out_0.rearrange("(p i) t -> p i t", i=PACK)
        out_codes = out_1[0].rearrange("p t r -> p (t r)").bitcast(I32)
        z, exps, sums, dealt, turned, grouped, y, result, rounded = {}, {}, {}, {}, {}, {}, {}, {}, {}

        def exponentials(k):
            z[k] = bank(k, [P, J])
            for cols in halves if k == 0 else [slice(0, J)]:
                nc.tensor.matmul_mx(
                    out=z[k][:, cols],
                    lhsT=xt_codes[:, 2 * P * k : 2 * P * (k + 1)].bitcast(E2M1),
                    lhsT_scale=xt_plane[:, P * k : P * (k + 1)],
                    rhs=picked_codes[:, cols].bitcast(E4M3),
                    rhs_scale=picked_plane[:, cols],
                    start=True,
                    stop=True,
                )
            minus_top = work.tile([P, 1], F32, name="minus_top")
            nc.vector.tensor_reduce(out=minus_top[:], in_=z[k][:], axis=AX.X, op=ALU.max, negate=True)
            exps[k] = work.tile([P, PACK, P], F32, name="exps")
            sums[k] = work.tile([P, 1], F32, name="sums")
            nc.scalar.activation(
                out=exps[k][:],
                in_=z[k][:].rearrange("p (q i) -> p i q", i=PACK),
                func=ACT.Exp,
                bias=minus_top[:],
                accum_out=sums[k][:],
            )

        def deal_targets(k):
            dealt[k] = work.tile([P, PACK, P], F32, name="dealt")
            nc.scalar.copy(
                out=dealt[k][:].rearrange("p i q -> p q i"), in_=targets[k][:].rearrange("p (q i) -> p q i", i=PACK)
            )

        def gaps(k):
            inverse = work.tile([P, 1], F32, name="inverse")
            nc.vector.reciprocal(out=inverse[:], in_=sums[k][:])
            gap = work.tile([P, PACK, P], F32, name="gap")
            nc.vector.scalar_tensor_tensor(
                out=gap[:], in0=exps[k][:], scalar=inverse[:], in1=dealt[k][:], op0=ALU.mult, op1=ALU.subtract
            )
            turned[k] = bank(TILES + k, [P, PACK, P])
            for i in range(PACK):
                nc.tensor.transpose(turned[k][:, i, :], gap[:, i, :], ident[:])

        def errors(k):
            grouped[k] = work.tile([P, P, PACK], BF16, name="grouped", align_bytes=64)
            nc.vector.tensor_tensor(
                out=grouped[k][:],
                in0=turned[k][:].rearrange("p i t -> p t i"),
                in1=fj_rows[:].unsqueeze(1).to_broadcast([P, P, PACK]),
                op=ALU.mult,
            )

        def back(k):
            dw_codes = work.tile([P, P], U32, name="dw_codes", align_bytes=64)
            dw_plane = work.tile([P, P], U8, name="dw_plane", align_bytes=64)
            nc.vector.quantize_mx(out=dw_codes[:].bitcast(E5M2), scales=dw_plane[:], in_=grouped[k][:].rearrange("p t i -> p (t i)"))
            if k < TILES - 1:
                whole = bank(k, [P, PACK, P])
                y[k] = [whole]
                slots = [whole[:, i, :] for i in range(PACK)]
            else:
                y[k] = [bank(k, [P, 2, P]), bank(k + 1, [P, 2, P])]
                slots = [y[k][i // 2][:, i % 2, :] for i in range(PACK)]
            for i in range(PACK):
                nc.tensor.matmul_mx(
                    out=slots[i],
                    lhsT=wo_dealt_codes[:, 2 * P * i : 2 * P * (i + 1)].bitcast(E2M1),
                    lhsT_scale=wo_dealt_plane[:, P * i : P * (i + 1)],
                    rhs=dw_codes[:].bitcast(E5M2),
                    rhs_scale=dw_plane[:],
                    start=True,
                    stop=True,
                )

        def store(k):
            result[k] = work.tile([P, PACK, P], F32, name="result")
            if k < TILES - 1:
                nc.scalar.copy(out=result[k][:], in_=y[k][0][:])
            else:
                nc.scalar.copy(out=result[k][:, 0:2, :], in_=y[k][0][:])
                nc.vector.tensor_copy(out=result[k][:, 2:4, :], in_=y[k][1][:])
            nc.sync.dma_start(out=out_rows[:, :, P * k : P * (k + 1)], in_=result[k][:])

        def rounding(k):
            rounded[k] = work.tile([P, P, PACK], BF16, name="rounded", align_bytes=64)
            nc.vector.tensor_copy(out=rounded[k][:], in_=result[k][:].rearrange("p i t -> p t i"))

        def planes(k):
            cols = slice(P * k, P * (k + 1))
            nc.vector.quantize_mx(
                out=y_codes[:, cols].bitcast(E4M3),
                scales=y_plane[:, cols],
                in_=rounded[k][:].rearrange("p t i -> p (t i)"),
            )
            if k % 2 == 1:
                pair = slice(P * (k - 1), P * (k + 1))
                nc.sync.dma_start(out=out_codes[:, pair], in_=y_codes[:, pair].bitcast(I32))

        for k in range(EARLY):
            deal_targets(k)
        for k in range(TILES):
            exponentials(k)
        for k in range(TILES):
            if k >= EARLY:
                deal_targets(k)
            gaps(k)
        for step in range(TILES + 1):
            if step < TILES:
                errors(step)
            if step >= 1:
                back(step - 1)
        for k in range(TILES):
            store(k)
            rounding(k)
        for k in range(TILES):
            planes(k)

        for q in range(4):
            queue = nc.sync if q % 2 == 0 else nc.scalar
            queue.dma_start(
                out=out_2[0, 4 * q : 4 * q + 4, :].bitcast(I32), in_=y_plane[32 * q : 32 * q + 4, :].bitcast(I32)
            )
